import numpy as np, ml_dtypes
CORES = [40,41,42,43,44,45,46,47]
N = 8
BF = ml_dtypes.bfloat16
def gentries(a):
    return np.ascontiguousarray(a.reshape(8, 16, -1).transpose(0, 2, 1)).reshape(8, -1)
def gtable(e):
    e = np.asarray(e); return np.ascontiguousarray(e.reshape(8, -1, 16).transpose(0, 2, 1)).reshape(128, -1).astype(np.int32)
V, R = 2048, 8
def family(rng, sizes, depth, pool, mix, fall=None):
    key = np.tile(np.arange(V), (N, 1)); lev = np.zeros(V, np.int64); comp = np.zeros(V, np.int64); via = [-1] * V; o = rng.permutation(V); a = 0
    for i in range(len(sizes)):
        s, D = int(sizes[i]), int(depth[i]); m = o[a:a + s]; a += s; comp[m] = i
        if s == 1: continue
        root = int(np.min(m)); m = m[m != root]; l = np.concatenate([np.arange(1, D + 1), rng.integers(1, D + 1, s - 1 - D)])
        if fall is not None and fall[i]: m = np.sort(m)[::-1]; l = np.sort(l)
        lev[m] = l
        at = [[root]] + [[] for k in range(D)]
        for c, k in zip(m.tolist(), l.tolist()): at[k].append(c)
        for k in range(1, D + 1):
            for c in at[k]:
                p = at[k - 1][int(rng.integers(len(at[k - 1])))]; w = [q for q in pool if q != via[p]]; q = w[int(rng.integers(len(w)))]
                key[q, c] = key[q, p]; via[c] = q
    for q in range(N if mix > 0 else 0):
        h = np.flatnonzero(key[q] == np.arange(V)); t = comp[h] * (R + 1) + lev[h]; keep = rng.random(h.size) >= mix
        hk, tk = h[keep], t[keep]; s = np.argsort(tk, kind="stable"); hk, tk = hk[s], tk[s]
        lo = np.searchsorted(tk, t, "left"); n = np.searchsorted(tk, t, "right") - lo; z = ~keep & (n > 0)
        to = h + 0; to[z] = hk[lo[z] + (rng.random(np.count_nonzero(z)) * n[z]).astype(np.int64)]
        jump = np.arange(V); jump[h] = to; key[q] = jump[key[q]]
    return key
def lay(rng, key, way):
    if way == 0: o = np.lexsort((rng.random(V), rng.permutation(V)[key]))
    elif way == 1: o = np.lexsort((np.arange(V), key))
    else: o = np.lexsort((-np.arange(V), -key))
    k = key[o]; s = np.ones(V, np.int64); s[1:] = k[1:] != k[:-1]
    e = np.append(np.flatnonzero(s)[1:], V) - 1; last = np.zeros(V, np.int64); last[o] = e[np.add.accumulate(s) - 1]
    return [o, s, last]
def pack(rng, keys, ways):
    a = np.array([[lay(rng, keys[g][q], ways[q, g]) for g in range(8)] for q in range(N)])
    return {"pm": np.stack([gtable(u) for u in a[:, :, 0]]), "en": np.stack([gtable(u) for u in a[:, :, 2]]), "st": np.ascontiguousarray(a[:, :, 1]).astype(np.int32)}
def depths(rng, s):
    top = np.minimum(R, s - 1); D = np.where(top > 0, 1 + (rng.random(s.size) * top).astype(np.int64), 0); i = np.argmax(s); D[i] = top[i]; return D
def some(rng):
    out = []
    for n in rng.choice(np.arange(6, 41), 8, replace=False):
        c = np.sort(rng.choice(V - 1, int(n) - 1, replace=False)) + 1; s = np.diff(np.concatenate([[0], c, [V]]))
        out.append(family(rng, s, depths(rng, s), list(range(N)), rng.choice([0.0, 0.05, 0.15])))
    return out
def setup_inputs(rng):
    return pack(rng, some(rng), np.zeros((N, 8), np.int64))
def setup_inputs_deep(rng):
    few = rng.permutation(8)[:4]; n = rng.choice(np.arange(V // (2 * (R + 1)), V // (R + 1) + 1), 8, replace=False); keys = []
    for g in range(8):
        m = int(n[g]); s = [R + 1] * m + [1] * (V - m * (R + 1)); pool = rng.permutation(N)[:2].tolist() if g in few else list(range(N))
        keys.append(family(rng, s, [R] * m + [0] * (V - m * (R + 1)), pool, 0.0, np.arange(len(s)) % 2 == 0))
    return pack(rng, keys, np.zeros((N, 8), np.int64))
def setup_inputs_ends(rng):
    keys = some(rng); w = rng.permutation(8); one = np.tile(np.arange(V), (N, 1))
    keys[w[0]][rng.integers(N)] = 0
    keys[w[1]] = one + 0
    keys[w[2]] = np.tile(rng.integers(0, 30, V), (N, 1))
    keys[w[3]] = one + 0; keys[w[3]][rng.integers(N)] = rng.integers(0, 3, V)
    x = np.concatenate([[0], 1 + rng.choice(V - 2, R - 1, replace=False), [V - 1]]); k = one + 0; ab = rng.permutation(N)[:2]
    for i in range(R): k[ab[i % 2], x[i + 1]] = x[i]
    keys[w[4]] = k
    return pack(rng, keys, np.zeros((N, 8), np.int64))
def setup_inputs_order(rng):
    return pack(rng, some(rng), rng.integers(1, 3, (N, 8)))
def setup_inputs_spread(rng):
    keys = []; half = int(rng.integers(8))
    for g in range(8):
        s = [1] * (V // 2 if g == half else 0); left = V - len(s)
        while left > 0:
            t = max(1, int(left * (0.3 + 0.4 * rng.random()))); s.append(t); left -= t
        s = np.array(s); keys.append(family(rng, s, depths(rng, s), list(range(N)) + [int(rng.integers(N))] * (3 * N), rng.choice([0.0, 0.3, 0.8])))
    return pack(rng, keys, np.zeros((N, 8), np.int64))
def hop(p, st, L):
    g = np.arange(8)[:, None]; M = L
    for q in range(N):
        s = st[q].reshape(-1); m = np.minimum.reduceat(L[g, p[q]].reshape(-1), np.flatnonzero(s))
        u = np.empty_like(L); u[g, p[q]] = m[np.add.accumulate(s) - 1].reshape(8, V); M = np.minimum(M, u)
    return M
def check_inputs(d):
    p = np.stack([gentries(a) for a in d["pm"]]); e = np.stack([gentries(a) for a in d["en"]]); s = d["st"]
    if not (np.sort(p, -1) == np.arange(V)).all(): return ["pm: every vertex once"]
    if not (((s == 0) | (s == 1)).all() and (s[:, :, 0] == 1).all()): return ["st: 0 and 1, beginning with 1"]
    bad = []; t = s.reshape(-1); last = ((np.append(np.flatnonzero(t)[1:], t.size) - 1) % V)[np.add.accumulate(t) - 1].reshape(N, 8, V)
    if not (np.take_along_axis(e, p, 2) == last).all(): bad.append("en: last places")
    L = np.tile(np.arange(V), (8, 1))
    for i in range(R): L = hop(p, s, L)
    if not (hop(p, s, L) == L).all(): bad.append("at most R steps to the smallest vertex")
    return bad
def reference(pm, en, st):
    p = np.stack([gentries(a) for a in pm]); L = np.tile(np.arange(V), (8, 1))
    while True:
        M = hop(p, st, L)
        if (M == L).all(): break
        L = M
    c = np.count_nonzero(L == np.arange(V), axis=1).reshape(8, 1)
    return {"y": np.stack([L for r in range(N)]).astype(np.float32), "cnt": np.stack([c for r in range(N)]).astype(np.float32)}

@@ -1,0 +1,283 @@
+from concourse.bass import DstId, RemoteDMATransfer
+from concourse.mybir import AluOpType as A, ActivationFunctionType as F
+
+V, R, BLK = 2048, 8, 128
+CFG = {
+    "pm": [("v", 704), ("s", 992), ("s", 352)],
+    "chunks": [(2, 4), (4, 2), (1, 3)],
+    "order": "G0 L0 G1 N0 G2 L1 N1 T0 L2 T1 C0 B0 N2 C1 T2 X0.0 C2 X0.1 B1 B2 X1.1 X1.0 X2.1 X2.0",
+    "last": "G0 L0 G1 N0 G2 L1 N1 L2 N2",
+    "copy": "vvs",
+    "evac": [[("s", 0, 3), ("v", 3, 3)], [("s", 0, 3), ("v", 3, 3)], [("v", 0, 2), ("s", 2, 2)]],
+}
+NBMAX = 6
+SCALE = 2.0 ** -16
+
+SCRATCH = {
+    "txa": ("dram", [8, 128, 32], "int32"), "rxa": ("dram", [8, 128, 32], "int32"),
+    "txb": ("dram", [8, 128, 16], "int32"), "rxb": ("dram", [8, 128, 16], "int32"),
+    "pmi": ("sbuf", [128, 128], "int32"), "eni": ("sbuf", [128, 128], "int32"),
+    "pmo": ("sbuf", [128, 128], "uint16"), "eno": ("sbuf", [128, 128], "uint16"),
+    "mask": ("sbuf", [128, V], "bfloat16"),
+    "win": ("sbuf", [128, V], "bfloat16"), "plc": ("sbuf", [128, V], "bfloat16"),
+    "seg": ("sbuf", [128, V], "bfloat16"), "upd": ("sbuf", [128, V], "bfloat16"),
+    "ones": ("sbuf", [128, 128], "bfloat16"), "ident": ("sbuf", [128, 128], "bfloat16"),
+    "identf": ("sbuf", [128, 128], "float32"), "ramp": ("sbuf", [128, 128], "bfloat16"),
+    "sel": ("sbuf", [128, 8], "bfloat16"), "spread": ("sbuf", [128, NBMAX * 128], "bfloat16"),
+    "rst": ("sbuf", [128, 8 * NBMAX], "bfloat16"), "horn": ("sbuf", [128, 112], "bfloat16"),
+    "low": ("sbuf", [128, 128], "bfloat16"), "row": ("sbuf", [128, V], "bfloat16"),
+    "clip": ("sbuf", [128, 112], "bfloat16"), "dec": ("sbuf", [128, 112], "float32"),
+    "land": ("sbuf", [128, 128], "float32"), "own": ("sbuf", [128, 128], "float32"),
+    "eq": ("sbuf", [128, 128], "bfloat16"), "lab": ("sbuf", [128, 128], "float32"),
+    "num": ("sbuf", [128, 4], "float32"),
+    "ps_b0": ("psum", [128, 512], "float32"), "ps_b1": ("psum", [128, 512], "float32"),
+    "ps_b2": ("psum", [128, 512], "float32"), "ps_b3": ("psum", [128, 512], "float32"),
+    "ps_s0": ("psum", [128, 512], "float32"), "ps_s1": ("psum", [128, 512], "float32"),
+    "ps_t0": ("psum", [128, 1024], "bfloat16"), "ps_t1": ("psum", [128, 1024], "bfloat16"),
+}
+REMOTE = ["arr_a", "arr_b", "arr_y", "sent"]
+SEMAPHORES = REMOTE + ["q%d" % i for i in range(140)]
+
+
+def emit(queues, ops, sems):
+    batches = {}
+    for i, o in enumerate(ops):
+        batches.setdefault(o["key"], []).append(i)
+    hist, obs, snap, used, waits = {}, {}, {}, {}, []
+    for i, o in enumerate(ops):
+        q, deps = o["q"], []
+        both = [(0, x) for x in o["r"]] + [(1, x) for x in o["w"]]
+        for kind, (b, c0, c1) in both:
+            for (j, d0, d1, w) in hist.get(b, []):
+                cross = b.startswith("ps_") and ops[j]["q"] != q
+                if not cross and (not (kind or w) or d1 <= c0 or c1 <= d0):
+                    continue
+                if ops[j]["key"] != o["key"]:
+                    deps.append(j)
+        for kind, (b, c0, c1) in both:
+            h = hist.setdefault(b, [])
+            if kind and not b.startswith("ps_"):
+                h[:] = [x for x in h if not (c0 <= x[1] and x[2] <= c1) or ops[x[0]]["key"] == o["key"]]
+            elif kind:
+                h[:] = [x for x in h if not (c0 <= x[1] and x[2] <= c1 and ops[x[0]]["q"] == q) or ops[x[0]]["key"] == o["key"]]
+                if len(h) > 120:
+                    h[:] = h[-120:]
+            h.append((i, c0, c1, kind))
+        seen = obs.setdefault(q, {})
+        need = []
+        for j in sorted(set(deps), reverse=True):
+            name, b = ops[j]["key"]
+            if seen.get(name, -1) >= b:
+                continue
+            need.append((name, b))
+            used[name] = True
+            for k in batches[(name, b)]:
+                for n2, b2 in snap[k].items():
+                    if seen.get(n2, -1) < b2:
+                        seen[n2] = b2
+            seen[name] = b
+        waits.append(need)
+        snap[i] = dict(seen)
+    keep = {}
+    for o in ops:
+        n = o["key"][0]
+        if (n in used or o["inc"] == 16) and n not in keep:
+            keep[n] = sems.pop(0)
+    level, total = {}, {}
+    for o in ops:
+        n, b = o["key"]
+        if n in keep:
+            total[n] = total.get(n, 0) + o["inc"]
+            level[(n, b)] = total[n]
+    done = {}
+    for i, o in enumerate(ops):
+        eng = queues[o["q"]]
+        for (s, v) in o["ext"]:
+            eng.wait_ge(s, v)
+        for kb in waits[i]:
+            eng.wait_ge(keep[kb[0]], level[kb])
+            done[kb[0]] = max(done.get(kb[0], 0), level[kb])
+        ins = o["f"]()
+        if o["key"][0] in keep:
+            ins.then_inc(keep[o["key"][0]], o["inc"])
+    for n in keep:
+        if done.get(n, 0) < total[n]:
+            queues["y"].wait_ge(keep[n], total[n])
+
+
+def rank_program(g, core, T, topo):
+    me = T.rank_of(core)
+    if me is None:
+        return
+    cores = list(T.cores)
+    peers = [cores[(me + k) % len(cores)] for k in range(1, len(cores))]
+    queues = {"g": g, "v": g.vector, "s": g.scalar, "t": g.tensor, "y": g.sync}
+    ops = []
+    uniq = [0]
+
+    def op(q, key, f, r=(), w=(), inc=1, ext=()):
+        if key is None:
+            uniq[0] += 1
+            key = ("u%d" % uniq[0], 0)
+        ops.append({"q": q, "key": key, "f": f, "r": list(r), "w": list(w), "inc": inc, "ext": list(ext)})
+
+    def dma(q, key, out, in_, r, w, ext=()):
+        op(q, (key, 0), lambda: queues[q].dma_start(out, in_), r, w, 16, ext)
+
+    def c(n, a=0, b=None):
+        return (n, a, V if b is None else b)
+
+    def dst(d):
+        rid, pid = topo.addr(d)[0:2]
+        return DstId(rid=rid, pnc=pid)
+
+    lo = 16 * me
+    dma("y", "h_pm", T.txa[:, 0:64, :], T.pm[:], [], [c("txa_pm")])
+    dma("s", "h_st", T.txa[:, 64:128, :], T.st[:], [], [c("txa_st")])
+    dma("y", "h_en", T.txb[:], T.en[:], [], [c("txb")])
+    dma("s", "o_pm", T.rxa[me, 0:64, :], T.pm[lo:lo + 16, :], [], [c("rxa_pm")])
+    dma("s", "o_st", T.rxa[me, 64:128, :], T.st[me:me + 1, :], [], [c("rxa_st")])
+    dma("y", "o_en", T.rxb[me], T.en[lo:lo + 16, :], [], [c("rxb")])
+
+    op("v", None, lambda: g.vector.memset(T.ones[:], 1.0), [], [c("ones")])
+    op("g", None, lambda: g.iota(T.ramp[:], [[1, 128]], 0, 0, allow_small_or_imprecise_dtypes=True), [], [c("ramp")])
+    op("g", None, lambda: g.affine_select(T.ident[:], T.ones[:], [[-1, 128]], A.is_equal, 0.0, 0, 1), [c("ones")], [c("ident")])
+    op("g", None, lambda: g.affine_select(T.sel[:], T.ones[:, 0:8], [[-16, 8]], A.is_equal, 0.0, 0, 1), [c("ones")], [c("sel")])
+
+    es = topo.engines(core, peers[0])[0::2]
+
+    def a2a(tx, rx, arr, r):
+        def f():
+            tr = [RemoteDMATransfer(dst_ids=[dst(d)], dma_engine_mask=1 << es[k], remote_sem=arr,
+                                    srcs=[tx[T.rank_of(d)]], dsts=[rx[me]]) for k, d in enumerate(peers)]
+            return g.remote_dma_fused(tr, local_sem=T.sem.sent)
+        op("g", ("none", 0), f, r, [])
+    a2a(T.txa, T.rxa, T.sem.arr_a, [c("txa_pm"), c("txa_st")])
+    a2a(T.txb, T.rxb, T.sem.arr_b, [c("txb")])
+    n_in = len(peers)
+
+    op("v", None, lambda: g.vector.memset(T.mask[:], 0.0), [], [c("mask")])
+
+    def ramp(e):
+        m = 2.0 ** max((e - 8 if e >= 8 else 7 - e) - 1, 0)
+        a = 0.0 if e == 8 else (-128.0 if e == 7 else (128.0 if e > 7 else -256.0))
+        return lambda: g.vector.tensor_scalar(T.win[:, 128 * e:128 * e + 128], T.ramp[:], m * SCALE, a * m * SCALE, A.mult, A.add)
+    for e in range(16):
+        op("v", ("w0", 0), ramp(e), [c("ramp")], [c("win", 128 * e, 128 * e + 128)])
+    op("v", ("k_a", 0), lambda: g.vector.memset(T.rst[:], 0.0), [], [c("rst")])
+    op("v", ("k_b", 0), lambda: g.vector.memset(T.rst[:, 0::8], 1.0), [], [c("rst")])
+
+    def spread(b):
+        return lambda: g.vector.tensor_scalar(T.spread[:, 128 * b:128 * b + 128], T.ones[:], T.ident[:, 8 * b + 7:8 * b + 8], None, A.mult)
+    for b in range(NBMAX):
+        op("v", ("spr", 0), spread(b), [c("ones"), c("ident")], [c("spread", 128 * b, 128 * b + 128)])
+    op("v", ("k_c", 0), lambda: g.vector.memset(T.horn[:], 2.0), [], [c("horn")])
+    op("v", ("k_d", 0), lambda: g.vector.memset(T.horn[:, 0::7], 0.0), [], [c("horn")])
+    op("v", ("k_e", 0), lambda: g.vector.memset(T.horn[:, 6::7], 1.0), [], [c("horn")])
+    op("v", ("k_f", 0), lambda: g.vector.tensor_copy(T.identf[:], T.ident[:]), [c("ident")], [c("identf")])
+
+    dma("y", "l_pm", T.pmi[:], T.rxa[:, 0:64, :], [c("rxa_pm")], [c("pmi")], [(T.sem.arr_a, n_in)])
+    dma("g", "l_st", T.mask[0:128:16, :], T.rxa[:, 64:128, :], [c("rxa_st")], [c("mask")], [(T.sem.arr_a, n_in)])
+    dma("y", "l_en", T.eni[:], T.rxb[:], [c("rxb")], [c("eni")], [(T.sem.arr_b, n_in)])
+    op("g", None, lambda: g.iota(T.own[:], [[0, 8], [128, 16]], 0, 1, allow_small_or_imprecise_dtypes=True), [], [c("own")])
+    op("v", None, lambda: g.vector.tensor_copy(T.pmo[:], T.pmi[:]), [c("pmi")], [c("pmo")])
+
+    starts, b0 = [], 0
+    for nv, ns in CFG["chunks"]:
+        starts.append(b0)
+        b0 += nv + ns
+    bank, banks = [0], {}
+
+    def copy(q, key, o, i, r, w):
+        f = (lambda: g.vector.tensor_copy(o, i)) if q == "v" else (lambda: g.scalar.activation(o, i, F.Copy))
+        op(q, key, f, r, w)
+
+    def gather(q, key, out, win, off, a, b):
+        copy(q, key, T[out][:, a:b], T[win][:, 0:V].indirect(T[off][:, a // 16:b // 16]), [c(win), c(off)], [c(out, a, b)])
+
+    def places(r):
+        a = 0
+        for k, (q, n) in enumerate(CFG["pm"]):
+            gather(q, ("p%d" % k, r), "plc", "win", "pmo", a, a + n)
+            a += n
+        a = 0
+        for k, (q, n) in enumerate(CFG["pm"]):
+            def f(a=a, n=n):
+                init = 0.0 if a == 0 else T.seg[:, a - 1:a]
+                return g.vector.tensor_tensor_scan(T.seg[:, a:a + n], T.mask[:, a:a + n], T.plc[:, a:a + n], init, A.add, A.min)
+            op("v", ("c%d" % k, r), f, [c("mask", a, a + n), c("plc", a, a + n)] + ([c("seg", a - 1, a)] if a else []), [c("seg", a, a + n)])
+            a += n
+
+    def stage(t, i, r, piece):
+        nv, ns = CFG["chunks"][i]
+        s, nb = starts[i], nv + ns
+        p, pt = "ps_s%d" % (i % 2), "ps_t%d" % (i % 2)
+        row = c("row", BLK * i, BLK * i + BLK)
+        if t == "G":
+            if nv:
+                gather("v", ("gv%d" % i, r), "upd", "seg", "eno", BLK * s, BLK * (s + nv))
+            if ns:
+                gather("s", ("gs%d" % i, r), "upd", "seg", "eno", BLK * (s + nv), BLK * (s + nb))
+        elif t == "L":
+            for b in range(nb):
+                v0 = BLK * (s + b)
+                op("t", ("l%d" % i, r), lambda b=b, v0=v0: g.tensor.matmul(T[p][:, 8 * b:8 * b + 8], T.upd[:, v0:v0 + BLK], T.sel[:], True, True),
+                   [c("upd", v0, v0 + BLK), c("sel")], [c(p, 8 * b, 8 * b + 8)])
+        elif t == "N":
+            op("v", ("n%d" % i, r), lambda: g.vector.tensor_tensor_scan(T.low[:, 8 * s:8 * (s + nb)], T.rst[:, 0:8 * nb], T[p][:, 0:8 * nb], 0.0, A.add, A.min),
+               [c("rst"), c(p, 0, 8 * nb)], [c("low", 8 * s, 8 * (s + nb))])
+        elif t == "T":
+            op("t", ("t%d" % i, r), lambda: g.tensor.transpose(T[pt][0:8 * nb, 0:BLK], T.low[:, 8 * s:8 * (s + nb)], T.ident[:]),
+               [c("low", 8 * s, 8 * (s + nb)), c("ident")], [c(pt, 0, BLK)])
+        elif t == "C":
+            copy(CFG["copy"][i], ("y%d" % i, r), T.row[0:8 * nb, BLK * i:BLK * i + BLK], T[pt][0:8 * nb, 0:BLK], [c(pt, 0, BLK)], [row])
+        elif t == "B":
+            for k, (q, e0, n) in enumerate(CFG["evac"][i]):
+                pb = banks[(i, k)] = "ps_b%d" % (bank[0] % 4)
+                bank[0] += 1
+                for b in range(n):
+                    op("t", ("b%d_%d" % (i, k), r),
+                       lambda b=b, e=e0 + b, pb=pb: g.tensor.matmul(T[pb][:, BLK * b:BLK * b + BLK], T.spread[0:8 * nb, BLK * e:BLK * e + BLK],
+                                                                    T.row[0:8 * nb, BLK * i:BLK * i + BLK], True, True),
+                       [c("spread"), row], [c(pb, BLK * b, BLK * b + BLK)])
+        elif t == "X":
+            q, e0, n = CFG["evac"][i][piece]
+            pb, v0 = banks[(i, piece)], BLK * (s + e0)
+            copy(q, ("x%d_%d" % (i, piece), r), T.win[:, v0:v0 + BLK * n], T[pb][:, 0:BLK * n], [c(pb, 0, BLK * n)], [c("win", v0, v0 + BLK * n)])
+
+    for r in range(R):
+        places(r)
+        if r == 0:
+            op("v", None, lambda: g.vector.tensor_copy(T.eno[:], T.eni[:]), [c("eni")], [c("eno")])
+        for tok in (CFG["order"] if r < R - 1 else CFG["last"]).split():
+            tk = tok[1:].split(".")
+            stage(tok[0], int(tk[0]), r, int(tk[1]) if len(tk) > 1 else None)
+
+    for k in range(7):
+        if k < 6:
+            lim = 256.0 * 2.0 ** k * SCALE
+            f = lambda k=k, lim=lim: g.vector.tensor_scalar(T.clip[:, k::7], T.low[:, 7::8], lim, -lim, A.min, A.max)
+        else:
+            f = lambda: g.vector.tensor_copy(T.clip[:, 6::7], T.low[:, 7::8])
+        op("v", ("clip", 0), f, [c("low")], [c("clip")])
+    op("v", ("dec", 0), lambda: g.vector.tensor_tensor_scan(T.dec[:], T.horn[:], T.clip[:], 0.0, A.mult, A.add), [c("horn"), c("clip")], [c("dec")])
+    l0 = 16 * me
+    mine = T.land[:, l0:l0 + 16]
+    op("v", ("lab", 0), lambda: g.vector.tensor_scalar(mine, T.dec[:, 6::7], 2.0 ** -6 / SCALE, 1024.0, A.mult, A.add), [c("dec")], [c("land", l0, l0 + 16)])
+
+    def bcast():
+        return g.remote_dma_fused([RemoteDMATransfer(dst_ids=[dst(d) for d in peers], dma_engine_mask=sum(1 << e for e in es), remote_sem=T.sem.arr_y,
+                                                     srcs=[mine], dsts=[mine for d in peers])], local_sem=T.sem.sent)
+    op("g", ("none", 1), bcast, [c("land", l0, l0 + 16)], [])
+    arr = [(T.sem.arr_y, len(es) * len(peers))]
+    op("t", ("fin_t", 0), lambda: g.tensor.transpose(T.ps_b0[:, 0:128], T.land[:], T.identf[:]), [c("land", l0, l0 + 16), c("identf")], [c("ps_b0", 0, 128)], 1, arr)
+    op("v", ("fin_e", 0), lambda: g.vector.tensor_tensor(T.eq[:], T.land[:], T.own[:], A.is_equal), [c("land", l0, l0 + 16), c("own")], [c("eq")], 1, arr)
+    copy("s", ("fin_l", 0), T.lab[:], T.ps_b0[:, 0:128], [c("ps_b0", 0, 128)], [c("lab")])
+    for b in range(16):
+        op("t", ("fin_n", 0), lambda b=b: g.tensor.matmul(T.ps_s0[0:8, 0:1], T.eq[:, b::16], T.ones[:, 0:1], b == 0, b == 15), [c("eq"), c("ones")], [c("ps_s0", 0, 1)])
+    copy("v", ("fin_c", 0), T.num[0:8, 0:1], T.ps_s0[0:8, 0:1], [c("ps_s0", 0, 1)], [c("num")])
+    dma("s", "st_y", T.y[:], T.lab[:], [c("lab")], [])
+    dma("y", "st_c", T.cnt[:], T.num[0:8, 0:1], [c("num")], [])
+
+    emit(queues, ops, [T.sem["q%d" % i] for i in range(140)])
+    g.wait_ge(T.sem.sent, 2 * n_in + len(es))

@@ -2,13 +2,16 @@ from concourse.bass import DstId, RemoteDMATransfer
 from concourse.mybir import AluOpType as A, ActivationFunctionType as F
 
 V, R, BLK = 2048, 8, 128
+PR = 64
 CFG = {
-    "pm": [("v", 704), ("s", 992), ("s", 352)],
+    "pm": [("v", 672), ("s", 928), ("s", 448)],
+    "pieces": [("s", 384, "v"), ("v", 512, "s"), ("s", 288, "s"), ("s", 288, "v"), ("s", 192, "v"), ("v", 384, "v")],
+    "odd": "g0 g1 b0 g5 g3 b1 g4 b3 b4 b5 x0 x3 g2 x4 x1 x5 b2 x2",
     "chunks": [(2, 4), (4, 2), (1, 3)],
-    "order": "G0 L0 G1 N0 G2 L1 N1 T0 L2 T1 C0 B0 N2 C1 T2 X0.0 C2 X0.1 B1 B2 X1.1 X1.0 X2.1 X2.0",
-    "last": "G0 L0 G1 N0 G2 L1 N1 L2 N2",
-    "copy": "vvs",
-    "evac": [[("s", 0, 3), ("v", 3, 3)], [("s", 0, 3), ("v", 3, 3)], [("v", 0, 2), ("s", 2, 2)]],
+    "order": "G0 L0 G1 L1 G2 N0 T0 L2 N1 T1 C0 B0 N2 T2 C1 B1 X0.0 X0.1 C2 X1.0 X1.1 B2 X2.0 X2.1",
+    "last": "G0 L0 G1 L1 G2 N0 L2 N1 N2",
+    "copy": "svv",
+    "evac": [[("v", 0, 3), ("s", 3, 3)], [("s", 0, 3), ("v", 3, 3)], [("s", 0, 2), ("v", 2, 2)]],
 }
 NBMAX = 6
 SCALE = 2.0 ** -16
@@ -18,14 +21,15 @@ SCRATCH = {
     "txb": ("dram", [8, 128, 16], "int32"), "rxb": ("dram", [8, 128, 16], "int32"),
     "pmi": ("sbuf", [128, 128], "int32"), "eni": ("sbuf", [128, 128], "int32"),
     "pmo": ("sbuf", [128, 128], "uint16"), "eno": ("sbuf", [128, 128], "uint16"),
-    "mask": ("sbuf", [128, V], "bfloat16"),
+    "mask": ("sbuf", [128, V], "bfloat16"), "maskall": ("sbuf", [128, V], "bfloat16"),
     "win": ("sbuf", [128, V], "bfloat16"), "plc": ("sbuf", [128, V], "bfloat16"),
     "seg": ("sbuf", [128, V], "bfloat16"), "upd": ("sbuf", [128, V], "bfloat16"),
     "ones": ("sbuf", [128, 128], "bfloat16"), "ident": ("sbuf", [128, 128], "bfloat16"),
     "identf": ("sbuf", [128, 128], "float32"), "ramp": ("sbuf", [128, 128], "bfloat16"),
-    "sel": ("sbuf", [128, 8], "bfloat16"), "spread": ("sbuf", [128, NBMAX * 128], "bfloat16"),
-    "rst": ("sbuf", [128, 8 * NBMAX], "bfloat16"), "horn": ("sbuf", [128, 112], "bfloat16"),
-    "low": ("sbuf", [128, 128], "bfloat16"), "row": ("sbuf", [128, V], "bfloat16"),
+    "sel": ("sbuf", [128, PR], "bfloat16"), "lanes": ("sbuf", [128, 128], "bfloat16"),
+    "spread": ("sbuf", [128, NBMAX * 128], "bfloat16"),
+    "rst": ("sbuf", [128, PR * NBMAX], "bfloat16"), "horn": ("sbuf", [128, 112], "bfloat16"),
+    "low": ("sbuf", [128, 16 * PR], "bfloat16"), "row": ("sbuf", [128, V], "bfloat16"),
     "clip": ("sbuf", [128, 112], "bfloat16"), "dec": ("sbuf", [128, 112], "float32"),
     "land": ("sbuf", [128, 128], "float32"), "own": ("sbuf", [128, 128], "float32"),
     "eq": ("sbuf", [128, 128], "bfloat16"), "lab": ("sbuf", [128, 128], "float32"),
@@ -142,7 +146,8 @@ def rank_program(g, core, T, topo):
     op("v", None, lambda: g.vector.memset(T.ones[:], 1.0), [], [c("ones")])
     op("g", None, lambda: g.iota(T.ramp[:], [[1, 128]], 0, 0, allow_small_or_imprecise_dtypes=True), [], [c("ramp")])
     op("g", None, lambda: g.affine_select(T.ident[:], T.ones[:], [[-1, 128]], A.is_equal, 0.0, 0, 1), [c("ones")], [c("ident")])
-    op("g", None, lambda: g.affine_select(T.sel[:], T.ones[:, 0:8], [[-16, 8]], A.is_equal, 0.0, 0, 1), [c("ones")], [c("sel")])
+    op("g", None, lambda: g.affine_select(T.sel[:], T.ones[:, 0:PR], [[-16, 8], [-1, 8]], A.is_equal, 0.0, 0, 1), [c("ones")], [c("sel")])
+    op("g", None, lambda: g.affine_select(T.lanes[:], T.ones[:], [[0, 8], [0, 2], [-16, 8]], A.is_equal, 0.0, 0, 1), [c("ones")], [c("lanes")])
 
     es = topo.engines(core, peers[0])[0::2]
 
@@ -165,20 +170,23 @@ def rank_program(g, core, T, topo):
     for e in range(16):
         op("v", ("w0", 0), ramp(e), [c("ramp")], [c("win", 128 * e, 128 * e + 128)])
     op("v", ("k_a", 0), lambda: g.vector.memset(T.rst[:], 0.0), [], [c("rst")])
-    op("v", ("k_b", 0), lambda: g.vector.memset(T.rst[:, 0::8], 1.0), [], [c("rst")])
+    op("v", ("k_b", 0), lambda: g.vector.memset(T.rst[:, 0::PR], 1.0), [], [c("rst")])
 
     def spread(b):
-        return lambda: g.vector.tensor_scalar(T.spread[:, 128 * b:128 * b + 128], T.ones[:], T.ident[:, 8 * b + 7:8 * b + 8], None, A.mult)
+        return lambda: g.vector.tensor_scalar(T.spread[:, 128 * b:128 * b + 128], T.ones[:], T.ident[:, b:b + 1], None, A.mult)
     for b in range(NBMAX):
         op("v", ("spr", 0), spread(b), [c("ones"), c("ident")], [c("spread", 128 * b, 128 * b + 128)])
     op("v", ("k_c", 0), lambda: g.vector.memset(T.horn[:], 2.0), [], [c("horn")])
     op("v", ("k_d", 0), lambda: g.vector.memset(T.horn[:, 0::7], 0.0), [], [c("horn")])
     op("v", ("k_e", 0), lambda: g.vector.memset(T.horn[:, 6::7], 1.0), [], [c("horn")])
     op("v", ("k_f", 0), lambda: g.vector.tensor_copy(T.identf[:], T.ident[:]), [c("ident")], [c("identf")])
+    op("v", None, lambda: g.vector.memset(T.maskall[:], 0.0), [], [c("maskall")])
 
     dma("y", "l_pm", T.pmi[:], T.rxa[:, 0:64, :], [c("rxa_pm")], [c("pmi")], [(T.sem.arr_a, n_in)])
     dma("g", "l_st", T.mask[0:128:16, :], T.rxa[:, 64:128, :], [c("rxa_st")], [c("mask")], [(T.sem.arr_a, n_in)])
     dma("y", "l_en", T.eni[:], T.rxb[:], [c("rxb")], [c("eni")], [(T.sem.arr_b, n_in)])
+    for i in range(8):
+        dma("y", "m_%d" % i, T.maskall[i:128:16, :], T.mask[0:128:16, :], [c("mask")], [("maskall", i, i + 1)])
     op("g", None, lambda: g.iota(T.own[:], [[0, 8], [128, 16]], 0, 1, allow_small_or_imprecise_dtypes=True), [], [c("own")])
     op("v", None, lambda: g.vector.tensor_copy(T.pmo[:], T.pmi[:]), [c("pmi")], [c("pmo")])
 
@@ -200,65 +208,82 @@ def rank_program(g, core, T, topo):
         for k, (q, n) in enumerate(CFG["pm"]):
             gather(q, ("p%d" % k, r), "plc", "win", "pmo", a, a + n)
             a += n
-        a = 0
+        a, m = 0, "mask" if r == 0 else "maskall"
         for k, (q, n) in enumerate(CFG["pm"]):
             def f(a=a, n=n):
                 init = 0.0 if a == 0 else T.seg[:, a - 1:a]
-                return g.vector.tensor_tensor_scan(T.seg[:, a:a + n], T.mask[:, a:a + n], T.plc[:, a:a + n], init, A.add, A.min)
-            op("v", ("c%d" % k, r), f, [c("mask", a, a + n), c("plc", a, a + n)] + ([c("seg", a - 1, a)] if a else []), [c("seg", a, a + n)])
+                return g.vector.tensor_tensor_scan(T.seg[:, a:a + n], T[m][:, a:a + n], T.plc[:, a:a + n], init, A.add, A.min)
+            op("v", ("c%d" % k, r), f, [c(m), c("plc", a, a + n)] + ([c("seg", a - 1, a)] if a else []), [c("seg", a, a + n)])
             a += n
 
-    def stage(t, i, r, piece):
+    def merge_stage(t, i, r, piece):
         nv, ns = CFG["chunks"][i]
         s, nb = starts[i], nv + ns
         p, pt = "ps_s%d" % (i % 2), "ps_t%d" % (i % 2)
-        row = c("row", BLK * i, BLK * i + BLK)
+        row, low = c("row", BLK * i, BLK * i + BLK), c("low", PR * s, PR * (s + nb))
         if t == "G":
-            if nv:
-                gather("v", ("gv%d" % i, r), "upd", "seg", "eno", BLK * s, BLK * (s + nv))
-            if ns:
-                gather("s", ("gs%d" % i, r), "upd", "seg", "eno", BLK * (s + nv), BLK * (s + nb))
+            gather("v", ("gv%d" % i, r), "upd", "seg", "eno", BLK * s, BLK * (s + nv))
+            gather("s", ("gs%d" % i, r), "upd", "seg", "eno", BLK * (s + nv), BLK * (s + nb))
         elif t == "L":
             for b in range(nb):
                 v0 = BLK * (s + b)
-                op("t", ("l%d" % i, r), lambda b=b, v0=v0: g.tensor.matmul(T[p][:, 8 * b:8 * b + 8], T.upd[:, v0:v0 + BLK], T.sel[:], True, True),
-                   [c("upd", v0, v0 + BLK), c("sel")], [c(p, 8 * b, 8 * b + 8)])
+                op("t", ("l%d" % i, r), lambda b=b, v0=v0: g.tensor.matmul(T[p][:, PR * b:PR * b + PR], T.upd[:, v0:v0 + BLK], T.sel[:], True, True),
+                   [c("upd", v0, v0 + BLK), c("sel")], [c(p, PR * b, PR * b + PR)])
         elif t == "N":
-            op("v", ("n%d" % i, r), lambda: g.vector.tensor_tensor_scan(T.low[:, 8 * s:8 * (s + nb)], T.rst[:, 0:8 * nb], T[p][:, 0:8 * nb], 0.0, A.add, A.min),
-               [c("rst"), c(p, 0, 8 * nb)], [c("low", 8 * s, 8 * (s + nb))])
+            op("v", ("n%d" % i, r), lambda: g.vector.tensor_tensor_scan(T.low[:, PR * s:PR * (s + nb)], T.rst[:, 0:PR * nb], T[p][:, 0:PR * nb], 0.0, A.add, A.min),
+               [c("rst"), c(p, 0, PR * nb)], [low])
         elif t == "T":
-            op("t", ("t%d" % i, r), lambda: g.tensor.transpose(T[pt][0:8 * nb, 0:BLK], T.low[:, 8 * s:8 * (s + nb)], T.ident[:]),
-               [c("low", 8 * s, 8 * (s + nb)), c("ident")], [c(pt, 0, BLK)])
+            op("t", ("t%d" % i, r), lambda: g.tensor.transpose(T[pt][0:nb, 0:BLK], T.low[:, PR * s + PR - 1:PR * (s + nb):PR], T.ident[:]),
+               [low, c("ident")], [c(pt, 0, BLK)])
         elif t == "C":
-            copy(CFG["copy"][i], ("y%d" % i, r), T.row[0:8 * nb, BLK * i:BLK * i + BLK], T[pt][0:8 * nb, 0:BLK], [c(pt, 0, BLK)], [row])
+            copy(CFG["copy"][i], ("y%d" % i, r), T.row[0:nb, BLK * i:BLK * i + BLK], T[pt][0:nb, 0:BLK], [c(pt, 0, BLK)], [row])
         elif t == "B":
             for k, (q, e0, n) in enumerate(CFG["evac"][i]):
                 pb = banks[(i, k)] = "ps_b%d" % (bank[0] % 4)
                 bank[0] += 1
                 for b in range(n):
                     op("t", ("b%d_%d" % (i, k), r),
-                       lambda b=b, e=e0 + b, pb=pb: g.tensor.matmul(T[pb][:, BLK * b:BLK * b + BLK], T.spread[0:8 * nb, BLK * e:BLK * e + BLK],
-                                                                    T.row[0:8 * nb, BLK * i:BLK * i + BLK], True, True),
+                       lambda b=b, e=e0 + b, pb=pb: g.tensor.matmul(T[pb][:, BLK * b:BLK * b + BLK], T.spread[0:nb, BLK * e:BLK * e + BLK],
+                                                                    T.row[0:nb, BLK * i:BLK * i + BLK], True, True),
                        [c("spread"), row], [c(pb, BLK * b, BLK * b + BLK)])
         elif t == "X":
             q, e0, n = CFG["evac"][i][piece]
             pb, v0 = banks[(i, piece)], BLK * (s + e0)
             copy(q, ("x%d_%d" % (i, piece), r), T.win[:, v0:v0 + BLK * n], T[pb][:, 0:BLK * n], [c(pb, 0, BLK * n)], [c("win", v0, v0 + BLK * n)])
 
+    pieces, a = [], 0
+    for (q, n, x) in CFG["pieces"]:
+        pieces.append((q, a, a + n, x, ("ps_b0", "ps_b1", "ps_b2", "ps_b3", "ps_s0", "ps_s1")[len(pieces)]))
+        a += n
+
+    def spread_stage(t, k, r):
+        q, a, b, x, pb = pieces[k]
+        if t == "g":
+            gather(q, ("og%d" % k, r), "upd", "seg", "eno", a, b)
+        elif t == "b":
+            op("t", ("ob%d" % k, r), lambda: g.tensor.matmul(T[pb][:, 0:b - a], T.lanes[:], T.upd[:, a:b], True, True),
+               [c("lanes"), c("upd", a, b)], [c(pb, 0, b - a)])
+        else:
+            copy(x, ("ox%d" % k, r), T.win[:, a:b], T[pb][:, 0:b - a], [c(pb, 0, b - a)], [c("win", a, b)])
+
     for r in range(R):
         places(r)
         if r == 0:
             op("v", None, lambda: g.vector.tensor_copy(T.eno[:], T.eni[:]), [c("eni")], [c("eno")])
-        for tok in (CFG["order"] if r < R - 1 else CFG["last"]).split():
-            tk = tok[1:].split(".")
-            stage(tok[0], int(tk[0]), r, int(tk[1]) if len(tk) > 1 else None)
+        if r % 2 == 0:
+            for tok in CFG["odd"].split():
+                spread_stage(tok[0], int(tok[1:]), r)
+        else:
+            for tok in (CFG["order"] if r < R - 1 else CFG["last"]).split():
+                tk = tok[1:].split(".")
+                merge_stage(tok[0], int(tk[0]), r, int(tk[1]) if len(tk) > 1 else None)
 
     for k in range(7):
         if k < 6:
             lim = 256.0 * 2.0 ** k * SCALE
-            f = lambda k=k, lim=lim: g.vector.tensor_scalar(T.clip[:, k::7], T.low[:, 7::8], lim, -lim, A.min, A.max)
+            f = lambda k=k, lim=lim: g.vector.tensor_scalar(T.clip[:, k::7], T.low[:, PR - 1::PR], lim, -lim, A.min, A.max)
         else:
-            f = lambda: g.vector.tensor_copy(T.clip[:, 6::7], T.low[:, 7::8])
+            f = lambda: g.vector.tensor_copy(T.clip[:, 6::7], T.low[:, PR - 1::PR])
         op("v", ("clip", 0), f, [c("low")], [c("clip")])
     op("v", ("dec", 0), lambda: g.vector.tensor_tensor_scan(T.dec[:], T.horn[:], T.clip[:], 0.0, A.mult, A.add), [c("horn"), c("clip")], [c("dec")])
     l0 = 16 * me

from concourse.bass import DstId, RemoteDMATransfer
from concourse.mybir import AluOpType as A, ActivationFunctionType as F

V, R, BLK = 2048, 8, 128
PR = 64
CFG = {
    "pm": [("v", 672), ("s", 928), ("s", 448)],
    "pieces": [("s", 384, "v"), ("v", 512, "s"), ("s", 288, "s"), ("s", 288, "v"), ("s", 192, "v"), ("v", 384, "v")],
    "odd": "g0 g1 b0 g5 g3 b1 g4 b3 b4 b5 x0 x3 g2 x4 x1 x5 b2 x2",
    "chunks": [(2, 4), (4, 2), (1, 3)],
    "order": "G0 L0 G1 L1 G2 N0 T0 L2 N1 T1 C0 B0 N2 T2 C1 B1 X0.0 X0.1 C2 X1.0 X1.1 B2 X2.0 X2.1",
    "last": "G0 L0 G1 L1 G2 N0 L2 N1 N2",
    "copy": "svv",
    "evac": [[("v", 0, 3), ("s", 3, 3)], [("s", 0, 3), ("v", 3, 3)], [("s", 0, 2), ("v", 2, 2)]],
}
NBMAX = 6
SCALE = 2.0 ** -16

SCRATCH = {
    "txa": ("dram", [8, 128, 32], "int32"), "rxa": ("dram", [8, 128, 32], "int32"),
    "txb": ("dram", [8, 128, 16], "int32"), "rxb": ("dram", [8, 128, 16], "int32"),
    "pmi": ("sbuf", [128, 128], "int32"), "eni": ("sbuf", [128, 128], "int32"),
    "pmo": ("sbuf", [128, 128], "uint16"), "eno": ("sbuf", [128, 128], "uint16"),
    "mask": ("sbuf", [128, V], "bfloat16"), "maskall": ("sbuf", [128, V], "bfloat16"),
    "win": ("sbuf", [128, V], "bfloat16"), "plc": ("sbuf", [128, V], "bfloat16"),
    "seg": ("sbuf", [128, V], "bfloat16"), "upd": ("sbuf", [128, V], "bfloat16"),
    "ones": ("sbuf", [128, 128], "bfloat16"), "ident": ("sbuf", [128, 128], "bfloat16"),
    "identf": ("sbuf", [128, 128], "float32"), "ramp": ("sbuf", [128, 128], "bfloat16"),
    "sel": ("sbuf", [128, PR], "bfloat16"), "lanes": ("sbuf", [128, 128], "bfloat16"),
    "spread": ("sbuf", [128, NBMAX * 128], "bfloat16"),
    "rst": ("sbuf", [128, PR * NBMAX], "bfloat16"), "horn": ("sbuf", [128, 112], "bfloat16"),
    "low": ("sbuf", [128, 16 * PR], "bfloat16"), "row": ("sbuf", [128, V], "bfloat16"),
    "clip": ("sbuf", [128, 112], "bfloat16"), "dec": ("sbuf", [128, 112], "float32"),
    "land": ("sbuf", [128, 128], "float32"), "own": ("sbuf", [128, 128], "float32"),
    "eq": ("sbuf", [128, 128], "bfloat16"), "lab": ("sbuf", [128, 128], "float32"),
    "num": ("sbuf", [128, 4], "float32"),
    "ps_b0": ("psum", [128, 512], "float32"), "ps_b1": ("psum", [128, 512], "float32"),
    "ps_b2": ("psum", [128, 512], "float32"), "ps_b3": ("psum", [128, 512], "float32"),
    "ps_s0": ("psum", [128, 512], "float32"), "ps_s1": ("psum", [128, 512], "float32"),
    "ps_t0": ("psum", [128, 1024], "bfloat16"), "ps_t1": ("psum", [128, 1024], "bfloat16"),
}
REMOTE = ["arr_a", "arr_b", "arr_y", "sent"]
SEMAPHORES = REMOTE + ["q%d" % i for i in range(140)]


def emit(queues, ops, sems):
    batches = {}
    for i, o in enumerate(ops):
        batches.setdefault(o["key"], []).append(i)
    hist, obs, snap, used, waits = {}, {}, {}, {}, []
    for i, o in enumerate(ops):
        q, deps = o["q"], []
        both = [(0, x) for x in o["r"]] + [(1, x) for x in o["w"]]
        for kind, (b, c0, c1) in both:
            for (j, d0, d1, w) in hist.get(b, []):
                cross = b.startswith("ps_") and ops[j]["q"] != q
                if not cross and (not (kind or w) or d1 <= c0 or c1 <= d0):
                    continue
                if ops[j]["key"] != o["key"]:
                    deps.append(j)
        for kind, (b, c0, c1) in both:
            h = hist.setdefault(b, [])
            if kind and not b.startswith("ps_"):
                h[:] = [x for x in h if not (c0 <= x[1] and x[2] <= c1) or ops[x[0]]["key"] == o["key"]]
            elif kind:
                h[:] = [x for x in h if not (c0 <= x[1] and x[2] <= c1 and ops[x[0]]["q"] == q) or ops[x[0]]["key"] == o["key"]]
                if len(h) > 120:
                    h[:] = h[-120:]
            h.append((i, c0, c1, kind))
        seen = obs.setdefault(q, {})
        need = []
        for j in sorted(set(deps), reverse=True):
            name, b = ops[j]["key"]
            if seen.get(name, -1) >= b:
                continue
            need.append((name, b))
            used[name] = True
            for k in batches[(name, b)]:
                for n2, b2 in snap[k].items():
                    if seen.get(n2, -1) < b2:
                        seen[n2] = b2
            seen[name] = b
        waits.append(need)
        snap[i] = dict(seen)
    keep = {}
    for o in ops:
        n = o["key"][0]
        if (n in used or o["inc"] == 16) and n not in keep:
            keep[n] = sems.pop(0)
    level, total = {}, {}
    for o in ops:
        n, b = o["key"]
        if n in keep:
            total[n] = total.get(n, 0) + o["inc"]
            level[(n, b)] = total[n]
    done = {}
    for i, o in enumerate(ops):
        eng = queues[o["q"]]
        for (s, v) in o["ext"]:
            eng.wait_ge(s, v)
        for kb in waits[i]:
            eng.wait_ge(keep[kb[0]], level[kb])
            done[kb[0]] = max(done.get(kb[0], 0), level[kb])
        ins = o["f"]()
        if o["key"][0] in keep:
            ins.then_inc(keep[o["key"][0]], o["inc"])
    for n in keep:
        if done.get(n, 0) < total[n]:
            queues["y"].wait_ge(keep[n], total[n])


def rank_program(g, core, T, topo):
    me = T.rank_of(core)
    if me is None:
        return
    cores = list(T.cores)
    peers = [cores[(me + k) % len(cores)] for k in range(1, len(cores))]
    queues = {"g": g, "v": g.vector, "s": g.scalar, "t": g.tensor, "y": g.sync}
    ops = []
    uniq = [0]

    def op(q, key, f, r=(), w=(), inc=1, ext=()):
        if key is None:
            uniq[0] += 1
            key = ("u%d" % uniq[0], 0)
        ops.append({"q": q, "key": key, "f": f, "r": list(r), "w": list(w), "inc": inc, "ext": list(ext)})

    def dma(q, key, out, in_, r, w, ext=()):
        op(q, (key, 0), lambda: queues[q].dma_start(out, in_), r, w, 16, ext)

    def c(n, a=0, b=None):
        return (n, a, V if b is None else b)

    def dst(d):
        rid, pid = topo.addr(d)[0:2]
        return DstId(rid=rid, pnc=pid)

    lo = 16 * me
    dma("y", "h_pm", T.txa[:, 0:64, :], T.pm[:], [], [c("txa_pm")])
    dma("s", "h_st", T.txa[:, 64:128, :], T.st[:], [], [c("txa_st")])
    dma("y", "h_en", T.txb[:], T.en[:], [], [c("txb")])
    dma("s", "o_pm", T.rxa[me, 0:64, :], T.pm[lo:lo + 16, :], [], [c("rxa_pm")])
    dma("s", "o_st", T.rxa[me, 64:128, :], T.st[me:me + 1, :], [], [c("rxa_st")])
    dma("y", "o_en", T.rxb[me], T.en[lo:lo + 16, :], [], [c("rxb")])

    op("v", None, lambda: g.vector.memset(T.ones[:], 1.0), [], [c("ones")])
    op("g", None, lambda: g.iota(T.ramp[:], [[1, 128]], 0, 0, allow_small_or_imprecise_dtypes=True), [], [c("ramp")])
    op("g", None, lambda: g.affine_select(T.ident[:], T.ones[:], [[-1, 128]], A.is_equal, 0.0, 0, 1), [c("ones")], [c("ident")])
    op("g", None, lambda: g.affine_select(T.sel[:], T.ones[:, 0:PR], [[-16, 8], [-1, 8]], A.is_equal, 0.0, 0, 1), [c("ones")], [c("sel")])
    op("g", None, lambda: g.affine_select(T.lanes[:], T.ones[:], [[0, 8], [0, 2], [-16, 8]], A.is_equal, 0.0, 0, 1), [c("ones")], [c("lanes")])

    es = topo.engines(core, peers[0])[0::2]

    def a2a(tx, rx, arr, r):
        def f():
            tr = [RemoteDMATransfer(dst_ids=[dst(d)], dma_engine_mask=1 << es[k], remote_sem=arr,
                                    srcs=[tx[T.rank_of(d)]], dsts=[rx[me]]) for k, d in enumerate(peers)]
            return g.remote_dma_fused(tr, local_sem=T.sem.sent)
        op("g", ("none", 0), f, r, [])
    a2a(T.txa, T.rxa, T.sem.arr_a, [c("txa_pm"), c("txa_st")])
    a2a(T.txb, T.rxb, T.sem.arr_b, [c("txb")])
    n_in = len(peers)

    op("v", None, lambda: g.vector.memset(T.mask[:], 0.0), [], [c("mask")])

    def ramp(e):
        m = 2.0 ** max((e - 8 if e >= 8 else 7 - e) - 1, 0)
        a = 0.0 if e == 8 else (-128.0 if e == 7 else (128.0 if e > 7 else -256.0))
        return lambda: g.vector.tensor_scalar(T.win[:, 128 * e:128 * e + 128], T.ramp[:], m * SCALE, a * m * SCALE, A.mult, A.add)
    for e in range(16):
        op("v", ("w0", 0), ramp(e), [c("ramp")], [c("win", 128 * e, 128 * e + 128)])
    op("v", ("k_a", 0), lambda: g.vector.memset(T.rst[:], 0.0), [], [c("rst")])
    op("v", ("k_b", 0), lambda: g.vector.memset(T.rst[:, 0::PR], 1.0), [], [c("rst")])

    def spread(b):
        return lambda: g.vector.tensor_scalar(T.spread[:, 128 * b:128 * b + 128], T.ones[:], T.ident[:, b:b + 1], None, A.mult)
    for b in range(NBMAX):
        op("v", ("spr", 0), spread(b), [c("ones"), c("ident")], [c("spread", 128 * b, 128 * b + 128)])
    op("v", ("k_c", 0), lambda: g.vector.memset(T.horn[:], 2.0), [], [c("horn")])
    op("v", ("k_d", 0), lambda: g.vector.memset(T.horn[:, 0::7], 0.0), [], [c("horn")])
    op("v", ("k_e", 0), lambda: g.vector.memset(T.horn[:, 6::7], 1.0), [], [c("horn")])
    op("v", ("k_f", 0), lambda: g.vector.tensor_copy(T.identf[:], T.ident[:]), [c("ident")], [c("identf")])
    op("v", None, lambda: g.vector.memset(T.maskall[:], 0.0), [], [c("maskall")])

    dma("y", "l_pm", T.pmi[:], T.rxa[:, 0:64, :], [c("rxa_pm")], [c("pmi")], [(T.sem.arr_a, n_in)])
    dma("g", "l_st", T.mask[0:128:16, :], T.rxa[:, 64:128, :], [c("rxa_st")], [c("mask")], [(T.sem.arr_a, n_in)])
    dma("y", "l_en", T.eni[:], T.rxb[:], [c("rxb")], [c("eni")], [(T.sem.arr_b, n_in)])
    for i in range(8):
        dma("y", "m_%d" % i, T.maskall[i:128:16, :], T.mask[0:128:16, :], [c("mask")], [("maskall", i, i + 1)])
    op("g", None, lambda: g.iota(T.own[:], [[0, 8], [128, 16]], 0, 1, allow_small_or_imprecise_dtypes=True), [], [c("own")])
    op("v", None, lambda: g.vector.tensor_copy(T.pmo[:], T.pmi[:]), [c("pmi")], [c("pmo")])

    starts, b0 = [], 0
    for nv, ns in CFG["chunks"]:
        starts.append(b0)
        b0 += nv + ns
    bank, banks = [0], {}

    def copy(q, key, o, i, r, w):
        f = (lambda: g.vector.tensor_copy(o, i)) if q == "v" else (lambda: g.scalar.activation(o, i, F.Copy))
        op(q, key, f, r, w)

    def gather(q, key, out, win, off, a, b):
        copy(q, key, T[out][:, a:b], T[win][:, 0:V].indirect(T[off][:, a // 16:b // 16]), [c(win), c(off)], [c(out, a, b)])

    def places(r):
        a = 0
        for k, (q, n) in enumerate(CFG["pm"]):
            gather(q, ("p%d" % k, r), "plc", "win", "pmo", a, a + n)
            a += n
        a, m = 0, "mask" if r == 0 else "maskall"
        for k, (q, n) in enumerate(CFG["pm"]):
            def f(a=a, n=n):
                init = 0.0 if a == 0 else T.seg[:, a - 1:a]
                return g.vector.tensor_tensor_scan(T.seg[:, a:a + n], T[m][:, a:a + n], T.plc[:, a:a + n], init, A.add, A.min)
            op("v", ("c%d" % k, r), f, [c(m), c("plc", a, a + n)] + ([c("seg", a - 1, a)] if a else []), [c("seg", a, a + n)])
            a += n

    def merge_stage(t, i, r, piece):
        nv, ns = CFG["chunks"][i]
        s, nb = starts[i], nv + ns
        p, pt = "ps_s%d" % (i % 2), "ps_t%d" % (i % 2)
        row, low = c("row", BLK * i, BLK * i + BLK), c("low", PR * s, PR * (s + nb))
        if t == "G":
            gather("v", ("gv%d" % i, r), "upd", "seg", "eno", BLK * s, BLK * (s + nv))
            gather("s", ("gs%d" % i, r), "upd", "seg", "eno", BLK * (s + nv), BLK * (s + nb))
        elif t == "L":
            for b in range(nb):
                v0 = BLK * (s + b)
                op("t", ("l%d" % i, r), lambda b=b, v0=v0: g.tensor.matmul(T[p][:, PR * b:PR * b + PR], T.upd[:, v0:v0 + BLK], T.sel[:], True, True),
                   [c("upd", v0, v0 + BLK), c("sel")], [c(p, PR * b, PR * b + PR)])
        elif t == "N":
            op("v", ("n%d" % i, r), lambda: g.vector.tensor_tensor_scan(T.low[:, PR * s:PR * (s + nb)], T.rst[:, 0:PR * nb], T[p][:, 0:PR * nb], 0.0, A.add, A.min),
               [c("rst"), c(p, 0, PR * nb)], [low])
        elif t == "T":
            op("t", ("t%d" % i, r), lambda: g.tensor.transpose(T[pt][0:nb, 0:BLK], T.low[:, PR * s + PR - 1:PR * (s + nb):PR], T.ident[:]),
               [low, c("ident")], [c(pt, 0, BLK)])
        elif t == "C":
            copy(CFG["copy"][i], ("y%d" % i, r), T.row[0:nb, BLK * i:BLK * i + BLK], T[pt][0:nb, 0:BLK], [c(pt, 0, BLK)], [row])
        elif t == "B":
            for k, (q, e0, n) in enumerate(CFG["evac"][i]):
                pb = banks[(i, k)] = "ps_b%d" % (bank[0] % 4)
                bank[0] += 1
                for b in range(n):
                    op("t", ("b%d_%d" % (i, k), r),
                       lambda b=b, e=e0 + b, pb=pb: g.tensor.matmul(T[pb][:, BLK * b:BLK * b + BLK], T.spread[0:nb, BLK * e:BLK * e + BLK],
                                                                    T.row[0:nb, BLK * i:BLK * i + BLK], True, True),
                       [c("spread"), row], [c(pb, BLK * b, BLK * b + BLK)])
        elif t == "X":
            q, e0, n = CFG["evac"][i][piece]
            pb, v0 = banks[(i, piece)], BLK * (s + e0)
            copy(q, ("x%d_%d" % (i, piece), r), T.win[:, v0:v0 + BLK * n], T[pb][:, 0:BLK * n], [c(pb, 0, BLK * n)], [c("win", v0, v0 + BLK * n)])

    pieces, a = [], 0
    for (q, n, x) in CFG["pieces"]:
        pieces.append((q, a, a + n, x, ("ps_b0", "ps_b1", "ps_b2", "ps_b3", "ps_s0", "ps_s1")[len(pieces)]))
        a += n

    def spread_stage(t, k, r):
        q, a, b, x, pb = pieces[k]
        if t == "g":
            gather(q, ("og%d" % k, r), "upd", "seg", "eno", a, b)
        elif t == "b":
            op("t", ("ob%d" % k, r), lambda: g.tensor.matmul(T[pb][:, 0:b - a], T.lanes[:], T.upd[:, a:b], True, True),
               [c("lanes"), c("upd", a, b)], [c(pb, 0, b - a)])
        else:
            copy(x, ("ox%d" % k, r), T.win[:, a:b], T[pb][:, 0:b - a], [c(pb, 0, b - a)], [c("win", a, b)])

    for r in range(R):
        places(r)
        if r == 0:
            op("v", None, lambda: g.vector.tensor_copy(T.eno[:], T.eni[:]), [c("eni")], [c("eno")])
        if r % 2 == 0:
            for tok in CFG["odd"].split():
                spread_stage(tok[0], int(tok[1:]), r)
        else:
            for tok in (CFG["order"] if r < R - 1 else CFG["last"]).split():
                tk = tok[1:].split(".")
                merge_stage(tok[0], int(tk[0]), r, int(tk[1]) if len(tk) > 1 else None)

    for k in range(7):
        if k < 6:
            lim = 256.0 * 2.0 ** k * SCALE
            f = lambda k=k, lim=lim: g.vector.tensor_scalar(T.clip[:, k::7], T.low[:, PR - 1::PR], lim, -lim, A.min, A.max)
        else:
            f = lambda: g.vector.tensor_copy(T.clip[:, 6::7], T.low[:, PR - 1::PR])
        op("v", ("clip", 0), f, [c("low")], [c("clip")])
    op("v", ("dec", 0), lambda: g.vector.tensor_tensor_scan(T.dec[:], T.horn[:], T.clip[:], 0.0, A.mult, A.add), [c("horn"), c("clip")], [c("dec")])
    l0 = 16 * me
    mine = T.land[:, l0:l0 + 16]
    op("v", ("lab", 0), lambda: g.vector.tensor_scalar(mine, T.dec[:, 6::7], 2.0 ** -6 / SCALE, 1024.0, A.mult, A.add), [c("dec")], [c("land", l0, l0 + 16)])

    def bcast():
        return g.remote_dma_fused([RemoteDMATransfer(dst_ids=[dst(d) for d in peers], dma_engine_mask=sum(1 << e for e in es), remote_sem=T.sem.arr_y,
                                                     srcs=[mine], dsts=[mine for d in peers])], local_sem=T.sem.sent)
    op("g", ("none", 1), bcast, [c("land", l0, l0 + 16)], [])
    arr = [(T.sem.arr_y, len(es) * len(peers))]
    op("t", ("fin_t", 0), lambda: g.tensor.transpose(T.ps_b0[:, 0:128], T.land[:], T.identf[:]), [c("land", l0, l0 + 16), c("identf")], [c("ps_b0", 0, 128)], 1, arr)
    op("v", ("fin_e", 0), lambda: g.vector.tensor_tensor(T.eq[:], T.land[:], T.own[:], A.is_equal), [c("land", l0, l0 + 16), c("own")], [c("eq")], 1, arr)
    copy("s", ("fin_l", 0), T.lab[:], T.ps_b0[:, 0:128], [c("ps_b0", 0, 128)], [c("lab")])
    for b in range(16):
        op("t", ("fin_n", 0), lambda b=b: g.tensor.matmul(T.ps_s0[0:8, 0:1], T.eq[:, b::16], T.ones[:, 0:1], b == 0, b == 15), [c("eq"), c("ones")], [c("ps_s0", 0, 1)])
    copy("v", ("fin_c", 0), T.num[0:8, 0:1], T.ps_s0[0:8, 0:1], [c("ps_s0", 0, 1)], [c("num")])
    dma("s", "st_y", T.y[:], T.lab[:], [c("lab")], [])
    dma("y", "st_c", T.cnt[:], T.num[0:8, 0:1], [c("num")], [])

    emit(queues, ops, [T.sem["q%d" % i] for i in range(140)])
    g.wait_ge(T.sem.sent, 2 * n_in + len(es))
